import numpy as np
import ml_dtypes


def mxq(x, axis, fmt="e4m3"):
    dtype, down = {"e4m3": (ml_dtypes.float8_e4m3fn, 7), "e5m2": (ml_dtypes.float8_e5m2, 14)}[fmt]
    v = np.moveaxis(np.asarray(x, np.float32).astype(ml_dtypes.bfloat16).astype(np.float64), axis, -1)
    blocks = v.reshape(v.shape[:-1] + (-1, 32))
    amax = np.abs(blocks).max(-1, keepdims=True)
    byte = np.maximum(np.where(amax > 0, np.frexp(amax)[1] - 1 + 127, 0) - down, 1)
    scale = np.exp2(byte - 127.0)
    codes = (blocks / scale).astype(np.float32).astype(dtype).astype(np.float64)
    return np.moveaxis((codes * scale).reshape(v.shape), -1, axis)


WIDE = False


def mx_kscale(k):
    if not WIDE:
        return np.ones(k)
    levels = np.array([10, -10, 5, -5, 0])
    if k % 512:
        return np.exp2(np.random.permutation(np.resize(levels, k // 32))).repeat(32)
    a = np.empty((k // 512, 16))
    for p in range(k // 512):
        a[p, :8] = np.random.permutation(np.resize(levels, 8))
        for g in range(8):
            far = levels[np.abs(levels - a[p, g]) >= 10]
            a[p, g + 8] = far[np.random.randint(len(far))]
    return np.exp2(a.ravel()).repeat(32)


def f64(x):
    return np.asarray(x).astype(np.float64)


def striped(idx):
    return np.tile(np.asarray(idx).reshape(-1, 16).T, (8, 1)).astype(np.uint16)


def unstriped(offs):
    return offs[:16].T.reshape(-1).astype(np.int64)


E2M1 = np.array([0.0, 0.5, 1.0, 1.5, 2.0, 3.0, 4.0, 6.0, -0.0, -0.5, -1.0, -1.5, -2.0, -3.0, -4.0, -6.0])


def pack_weight(w, fmt):
    k, n = w.shape
    w = f64(np.asarray(w, np.float32).astype(ml_dtypes.bfloat16)).reshape(k // 32, 32, n)
    amax = np.abs(w).max(1)
    if fmt == "e4m3":
        byte = np.frexp(amax)[1] - 1 + 127 - 7
    else:
        mant, ex = np.frexp(amax / 6.0)
        byte = np.where(mant > 0.5, ex, ex - 1) + 127
    byte = np.clip(np.where(amax > 0, byte, 1), 1, 254)
    scaled = (w * np.exp2(127.0 - byte)[:, None, :]).reshape(k, n).astype(np.float32)
    by_word = np.ascontiguousarray(scaled.reshape(k // 512, 128, 4, n).transpose(0, 1, 3, 2))
    if fmt == "e4m3":
        words = by_word.astype(ml_dtypes.float8_e4m3fn).view(np.uint8)
    else:
        c = by_word.astype(ml_dtypes.float4_e2m1fn).view(np.uint8) & 0xF
        words = (c[..., 0::2] | (c[..., 1::2] << 4)).reshape(k // 512, 128, 2 * n)
    return np.ascontiguousarray(words), np.ascontiguousarray(byte.astype(np.uint8).reshape(k // 512, 16, n))


def unpack_weight(words, scales, fmt):
    g, _, n = scales.shape
    words = np.ascontiguousarray(words).reshape(g, 128, n, -1)
    if fmt == "e4m3":
        vals = words.view(ml_dtypes.float8_e4m3fn).astype(np.float64)
    else:
        nib = np.empty((g, 128, n, 4), np.uint8)
        nib[..., 0::2] = words & 0xF
        nib[..., 1::2] = words >> 4
        vals = E2M1[nib]
    vals = vals * np.repeat(np.exp2(scales.astype(np.float64) - 127.0), 8, axis=1)[..., None]
    return vals.transpose(0, 1, 3, 2).reshape(g * 512, n)


def bf(x):
    return np.asarray(x, np.float32).astype(ml_dtypes.bfloat16)


def planes(Y):
    r, m = Y.shape
    b = f64(bf(Y)).reshape(r // 32, 32, m)
    amax = np.abs(b).max(1)
    byte = np.clip(np.where(amax > 0, np.frexp(amax)[1] - 1 + 127 - 7, 1), 1, 254)
    codes = (b * np.exp2(127.0 - byte)[:, None, :]).reshape(r, m).astype(np.float32).astype(ml_dtypes.float8_e4m3fn).view(np.uint8)
    words = codes.reshape(r // 512, 128, 4, m).transpose(0, 1, 3, 2)
    return np.ascontiguousarray(words), np.ascontiguousarray(byte.astype(np.uint8).reshape(r // 512, 16, m))


C, I, T, L, N = 2048, 512, 512, 512, 512


def setup_inputs():
    n = np.random.standard_normal
    idx = np.random.permutation(C)[:I]
    fi = mx_kscale(I)
    fl = mx_kscale(L)
    ti = np.ones(C)
    ti[idx] = fi
    wp = pack_weight(n((I, N)) * 1 / np.sqrt(I) * fi[:, None], "e4m3")
    cxp = pack_weight(n((L, T)) / fl[:, None], "e2m1")
    wcp = pack_weight(n((L, N)) * 1 / np.sqrt(L) * fl[:, None], "e4m3")
    return {
        "xt": (n((T, C)) / ti).astype(np.float32),
        "w_words": wp[0],
        "w_scales": wp[1],
        "cx_words": cxp[0],
        "cx_scales": cxp[1],
        "wc_words": wcp[0],
        "wc_scales": wcp[1],
        "offs": striped(idx),
    }


def reference(xt, w_words, w_scales, cx_words, cx_scales, wc_words, wc_scales, offs):
    idx = unstriped(offs)
    wu = unpack_weight(w_words, w_scales, "e4m3")
    cxu = unpack_weight(cx_words, cx_scales, "e2m1")
    wcu = unpack_weight(wc_words, wc_scales, "e4m3")
    xs = f64(xt)[:, idx].T
    xsq = mxq(xs, 0, "e4m3")
    a1 = wu.T @ xsq
    b1 = wcu.T @ cxu
    y = np.maximum(a1, 0.0) * b1
    words, scales = planes(y)
    return y, words, scales

@@ -1,0 +1,125 @@
+from contextlib import ExitStack
+
+import concourse.mybir as mybir
+from concourse.masks import make_identity
+
+C, I, T, L, N = 2048, 512, 512, 512, 512
+FLOPS = 2 * N * T * (I + L)
+
+F32 = mybir.dt.float32
+BF16 = mybir.dt.bfloat16
+I32 = mybir.dt.int32
+U16 = mybir.dt.uint16
+U8 = mybir.dt.uint8
+E4M3 = mybir.dt.float8_e4m3fn_x4
+E2M1 = mybir.dt.float4_e2m1fn_x4
+MAX = mybir.AluOpType.max
+MULT = mybir.AluOpType.mult
+
+P = 128
+PACK = 4
+TILES = T // P
+
+
+def tile_list_features_by_list_pl_kernel(tc, xt, w_words, w_scales, cx_words, cx_scales, wc_words, wc_scales, offs,
+                                            out_0, out_1, out_2):
+    nc = tc.nc
+    with ExitStack() as ctx:
+        keep = ctx.enter_context(tc.tile_pool(name="keep", bufs=1))
+        ring = ctx.enter_context(tc.tile_pool(name="ring", bufs=4))
+        ps_b = ctx.enter_context(tc.psum_pool(name="ps_b", bufs=4))
+        ps_x = ctx.enter_context(tc.psum_pool(name="ps_x", bufs=2))
+        ps_a = ctx.enter_context(tc.psum_pool(name="ps_a", bufs=2))
+
+        offsets = keep.tile([P, I // 16], U16, name="offsets")
+        nc.sync.dma_start(offsets[:], offs)
+
+        def load_words(name, words):
+            tile = keep.tile([P, words.shape[1] // 4], I32, name=name, align_bytes=64)
+            nc.sync.dma_start(tile[:], words.bitcast(I32))
+            return tile
+
+        staged = keep.tile([P, 3, 4, P], I32, name="staged")
+        for k, scales in enumerate((wc_scales, w_scales, cx_scales)):
+            nc.sync.dma_start(staged[0:P:32, k, :, :], scales[0].bitcast(I32).rearrange("(q r) c -> q r c", r=4))
+        wc_raw = load_words("wc_raw", wc_words[0].rearrange("p n r -> p (n r)"))
+        cx_w = load_words("cx_w", cx_words[0])
+        w_raw = load_words("w_raw", w_words[0].rearrange("p n r -> p (n r)"))
+        x_tiles = []
+        for tt in range(TILES):
+            x_tile = keep.tile([P, C], F32, name=f"x{tt}")
+            nc.sync.dma_start(x_tile[:], xt[tt * P:(tt + 1) * P, :])
+            x_tiles.append(x_tile)
+
+        planes = keep.tile([P, 3, N], U8, name="planes", align_bytes=64)
+        nc.vector.memset(planes[:].bitcast(I32), 0)
+        for r in range(4):
+            nc.scalar.dma_start(planes[:].bitcast(I32)[r:P:32, :, :], staged[0:P:32, :, r, :])
+        cx_s = planes[:, 2, :]
+
+        ident = keep.tile([P, P], F32, name="ident")
+        make_identity(nc, ident[:])
+
+        def deal(name, raw, dtype, run):
+            dealt = keep.tile([P, N], dtype, name=name, align_bytes=64)
+            nc.vector.tensor_copy(
+                out=dealt[:].rearrange("p (j a b) -> p a j b", j=PACK, b=run),
+                in_=raw.rearrange("p (a b j) -> p a j b", j=PACK, b=run))
+            return dealt
+
+        wc_d = deal("wc_d", wc_raw[:], I32, 4)
+        wc_s = deal("wc_s", planes[:, 0, :], U8, 16)
+        w_d = deal("w_d", w_raw[:], I32, 4)
+        w_s = deal("w_s", planes[:, 1, :], U8, 16)
+
+        cx_bytes = cx_w[:].bitcast(U8)
+        b_sb = []
+        for tt in range(TILES):
+            acc = ps_b.tile([P, PACK, P], F32, name="acc_b")
+            for j in range(PACK):
+                nc.tensor.matmul_mx(
+                    out=acc[:, j, :],
+                    lhsT=wc_d[:, j * P:(j + 1) * P].bitcast(E4M3), lhsT_scale=wc_s[:, j * P:(j + 1) * P],
+                    rhs=cx_bytes[:, 2 * tt * P:2 * (tt + 1) * P].bitcast(E2M1), rhs_scale=cx_s[:, tt * P:(tt + 1) * P],
+                    start=True, stop=True)
+            b_tile = keep.tile([P, PACK, P], F32, name=f"b{tt}")
+            nc.scalar.copy(out=b_tile[:], in_=acc[:])
+            b_sb.append(b_tile)
+
+        y_scales = keep.tile([P, T], U8, name="y_scales", align_bytes=64)
+        out_rows = out_0.rearrange("(p j) t -> p j t", j=PACK)
+        out_words = out_1[0].rearrange("p t r -> p (t r)").bitcast(I32)
+
+        for tt in range(TILES):
+            cols = slice(tt * P, (tt + 1) * P)
+            picked = ring.tile([P, I], BF16, name="picked")
+            nc.vector.tensor_copy(picked[:], x_tiles[tt][:].indirect(offsets[:]))
+            pairs = picked[:].bitcast(F32)
+            turned = ps_x.tile([P, 2, P], F32, name="turned")
+            for u in range(2):
+                nc.tensor.transpose(turned[:, u, :], pairs[:, u::2], ident[:])
+            grouped = ring.tile([P, P * PACK], BF16, name="grouped", align_bytes=64)
+            nc.scalar.copy(out=grouped[:].bitcast(F32).rearrange("p (t u) -> p t u", u=2),
+                           in_=turned[:].rearrange("p u t -> p t u"))
+            x_codes = ring.tile([P, P], I32, name="x_codes", align_bytes=64)
+            x_scales = ring.tile([P, P], U8, name="x_scales", align_bytes=64)
+            nc.vector.quantize_mx(out=x_codes[:].bitcast(E4M3), scales=x_scales[:], in_=grouped[:])
+            acc = ps_a.tile([P, PACK, P], F32, name="acc_a")
+            for j in range(PACK):
+                nc.tensor.matmul_mx(
+                    out=acc[:, j, :],
+                    lhsT=w_d[:, j * P:(j + 1) * P].bitcast(E4M3), lhsT_scale=w_s[:, j * P:(j + 1) * P],
+                    rhs=x_codes[:].bitcast(E4M3), rhs_scale=x_scales[:],
+                    start=True, stop=True)
+            y = ring.tile([P, PACK, P], F32, name="y")
+            nc.vector.scalar_tensor_tensor(out=y[:], in0=acc[:], scalar=0.0, in1=b_sb[tt][:], op0=MAX, op1=MULT)
+            nc.sync.dma_start(out_rows[:, :, cols], y[:])
+            y_grouped = ring.tile([P, P * PACK], BF16, name="y_grouped", align_bytes=64)
+            nc.scalar.copy(out=y_grouped[:].rearrange("p (t j) -> p t j", j=PACK), in_=y[:].rearrange("p j t -> p t j"))
+            y_codes = ring.tile([P, P], I32, name="y_codes", align_bytes=64)
+            nc.vector.quantize_mx(out=y_codes[:].bitcast(E4M3), scales=y_scales[:, cols], in_=y_grouped[:])
+            nc.sync.dma_start(out_words[:, cols], y_codes[:])
+
+        for q in range(4):
+            queue = nc.sync if q % 2 == 0 else nc.scalar
+            queue.dma_start(out_2[0, 4 * q:4 * q + 4, :].bitcast(I32), y_scales[32 * q:32 * q + 4, :].bitcast(I32))

@@ -26,28 +26,26 @@ def tile_list_features_by_list_pl_kernel(tc, xt, w_words, w_scales, cx_words, cx
     nc = tc.nc
     with ExitStack() as ctx:
         keep = ctx.enter_context(tc.tile_pool(name="keep", bufs=1))
-        ring = ctx.enter_context(tc.tile_pool(name="ring", bufs=4))
-        ps_b = ctx.enter_context(tc.psum_pool(name="ps_b", bufs=4))
-        ps_x = ctx.enter_context(tc.psum_pool(name="ps_x", bufs=2))
+        ring = ctx.enter_context(tc.tile_pool(name="ring", bufs=2))
+        ps_x = ctx.enter_context(tc.psum_pool(name="ps_x", bufs=1))
         ps_a = ctx.enter_context(tc.psum_pool(name="ps_a", bufs=2))
-
-        offsets = keep.tile([P, I // 16], U16, name="offsets")
-        nc.sync.dma_start(offsets[:], offs)
 
         def load_words(name, words):
             tile = keep.tile([P, words.shape[1] // 4], I32, name=name, align_bytes=64)
             nc.sync.dma_start(tile[:], words.bitcast(I32))
             return tile
 
-        staged = keep.tile([P, 3, 4, P], I32, name="staged")
-        for k, scales in enumerate((wc_scales, w_scales, cx_scales)):
-            nc.sync.dma_start(staged[0:P:32, k, :, :], scales[0].bitcast(I32).rearrange("(q r) c -> q r c", r=4))
         wc_raw = load_words("wc_raw", wc_words[0].rearrange("p n r -> p (n r)"))
         cx_w = load_words("cx_w", cx_words[0])
         w_raw = load_words("w_raw", w_words[0].rearrange("p n r -> p (n r)"))
+        offsets = keep.tile([P, I // 16], U16, name="offsets")
+        nc.sync.dma_start(offsets[:], offs)
+        staged = keep.tile([P, 3, 4, P], I32, name="staged")
+        for k, scales in enumerate((wc_scales, w_scales, cx_scales)):
+            nc.sync.dma_start(staged[0:P:32, k, :, :], scales[0].bitcast(I32).rearrange("(q r) c -> q r c", r=4))
         x_tiles = []
         for tt in range(TILES):
-            x_tile = keep.tile([P, C], F32, name=f"x{tt}")
+            x_tile = keep.tile([P, C], F32, name=f"x{tt}", tag=f"x{tt}", align_bytes=64)
             nc.sync.dma_start(x_tile[:], xt[tt * P:(tt + 1) * P, :])
             x_tiles.append(x_tile)
 
@@ -73,35 +71,36 @@ def tile_list_features_by_list_pl_kernel(tc, xt, w_words, w_scales, cx_words, cx
         w_s = deal("w_s", planes[:, 1, :], U8, 16)
 
         cx_bytes = cx_w[:].bitcast(U8)
-        b_sb = []
-        for tt in range(TILES):
-            acc = ps_b.tile([P, PACK, P], F32, name="acc_b")
+        y_scales = keep.tile([P, T], U8, name="y_scales", align_bytes=64)
+        out_rows = out_0.rearrange("(p j) t -> p j t", j=PACK)
+        out_words = out_1[0].rearrange("p t r -> p (t r)").bitcast(I32)
+
+        def pick(tt):
+            picked = keep.tile([P, I], BF16, name="picked", tag=f"picked{tt}", align_bytes=64)
+            nc.vector.tensor_copy(picked[:], x_tiles[tt][:].indirect(offsets[:]))
+            pairs = picked[:].bitcast(F32)
+            turned = ps_x.tile([P, 2, P], F32, name="turned", tag=f"bank{tt + 1}")
+            for u in range(2):
+                nc.tensor.transpose(turned[:, u, :], pairs[:, u::2], ident[:])
+            grouped = keep.tile([P, P * PACK], BF16, name="grouped", tag=f"grouped{tt}", align_bytes=64)
+            nc.scalar.copy(out=grouped[:].bitcast(F32).rearrange("p (t u) -> p t u", u=2),
+                           in_=turned[:].rearrange("p u t -> p t u"))
+            return grouped
+
+        def context(tt):
+            acc = ps_x.tile([P, PACK, P], F32, name="acc_b", tag=f"bank{tt}")
             for j in range(PACK):
                 nc.tensor.matmul_mx(
                     out=acc[:, j, :],
                     lhsT=wc_d[:, j * P:(j + 1) * P].bitcast(E4M3), lhsT_scale=wc_s[:, j * P:(j + 1) * P],
                     rhs=cx_bytes[:, 2 * tt * P:2 * (tt + 1) * P].bitcast(E2M1), rhs_scale=cx_s[:, tt * P:(tt + 1) * P],
                     start=True, stop=True)
-            b_tile = keep.tile([P, PACK, P], F32, name=f"b{tt}")
+            b_tile = keep.tile([P, PACK, P], F32, name=f"b{tt}", tag=f"b{tt}", align_bytes=64)
             nc.scalar.copy(out=b_tile[:], in_=acc[:])
-            b_sb.append(b_tile)
+            return b_tile
 
-        y_scales = keep.tile([P, T], U8, name="y_scales", align_bytes=64)
-        out_rows = out_0.rearrange("(p j) t -> p j t", j=PACK)
-        out_words = out_1[0].rearrange("p t r -> p (t r)").bitcast(I32)
-
-        for tt in range(TILES):
-            cols = slice(tt * P, (tt + 1) * P)
-            picked = ring.tile([P, I], BF16, name="picked")
-            nc.vector.tensor_copy(picked[:], x_tiles[tt][:].indirect(offsets[:]))
-            pairs = picked[:].bitcast(F32)
-            turned = ps_x.tile([P, 2, P], F32, name="turned")
-            for u in range(2):
-                nc.tensor.transpose(turned[:, u, :], pairs[:, u::2], ident[:])
-            grouped = ring.tile([P, P * PACK], BF16, name="grouped", align_bytes=64)
-            nc.scalar.copy(out=grouped[:].bitcast(F32).rearrange("p (t u) -> p t u", u=2),
-                           in_=turned[:].rearrange("p u t -> p t u"))
-            x_codes = ring.tile([P, P], I32, name="x_codes", align_bytes=64)
+        def multiply(tt, grouped):
+            x_codes = keep.tile([P, P], I32, name="x_codes", tag=f"x{tt + 1}", align_bytes=64)
             x_scales = ring.tile([P, P], U8, name="x_scales", align_bytes=64)
             nc.vector.quantize_mx(out=x_codes[:].bitcast(E4M3), scales=x_scales[:], in_=grouped[:])
             acc = ps_a.tile([P, PACK, P], F32, name="acc_a")
@@ -111,14 +110,45 @@ def tile_list_features_by_list_pl_kernel(tc, xt, w_words, w_scales, cx_words, cx
                     lhsT=w_d[:, j * P:(j + 1) * P].bitcast(E4M3), lhsT_scale=w_s[:, j * P:(j + 1) * P],
                     rhs=x_codes[:].bitcast(E4M3), rhs_scale=x_scales[:],
                     start=True, stop=True)
-            y = ring.tile([P, PACK, P], F32, name="y")
-            nc.vector.scalar_tensor_tensor(out=y[:], in0=acc[:], scalar=0.0, in1=b_sb[tt][:], op0=MAX, op1=MULT)
-            nc.sync.dma_start(out_rows[:, :, cols], y[:])
-            y_grouped = ring.tile([P, P * PACK], BF16, name="y_grouped", align_bytes=64)
-            nc.scalar.copy(out=y_grouped[:].rearrange("p (t j) -> p t j", j=PACK), in_=y[:].rearrange("p j t -> p t j"))
-            y_codes = ring.tile([P, P], I32, name="y_codes", align_bytes=64)
-            nc.vector.quantize_mx(out=y_codes[:].bitcast(E4M3), scales=y_scales[:, cols], in_=y_grouped[:])
-            nc.sync.dma_start(out_words[:, cols], y_codes[:])
+            return acc
+
+        def combine(tt, acc, b_tile, pieces):
+            y = keep.tile([P, PACK, P], F32, name="y", tag=f"grouped{tt + 1}", align_bytes=64)
+            y_grouped = keep.tile([P, P * PACK], BF16, name="y_grouped", tag=f"picked{tt + 2}", align_bytes=64)
+            width = P // pieces
+            for h in range(pieces):
+                part = slice(h * width, (h + 1) * width)
+                nc.vector.scalar_tensor_tensor(out=y[:, :, part], in0=acc[:, :, part], scalar=0.0, in1=b_tile[:, :, part],
+                                               op0=MAX, op1=MULT)
+                first = h * width
+                nc.scalar.copy(out=y_grouped[:, PACK * first:PACK * (first + width)].rearrange("p (t j) -> p t j", j=PACK),
+                               in_=y[:, :, part].rearrange("p j t -> p t j"))
+            nc.sync.dma_start(out_rows[:, :, tt * P:(tt + 1) * P], y[:])
+            return y_grouped
+
+        def hand_on(tt, y_grouped, pieces):
+            y_codes = keep.tile([P, P], I32, name="y_codes", tag=f"b{tt + 1}", align_bytes=64)
+            width = P // pieces
+            for first in range(0, P, width):
+                nc.vector.quantize_mx(out=y_codes[:, first:first + width].bitcast(E4M3),
+                                      scales=y_scales[:, tt * P + first:tt * P + first + width],
+                                      in_=y_grouped[:, PACK * first:PACK * (first + width)])
+            nc.sync.dma_start(out_words[:, tt * P:(tt + 1) * P], y_codes[:])
+
+        grouped, b_tiles, accs, rounded = {}, {}, {}, {}
+        for step in range(TILES + 3):
+            if step < TILES:
+                b_tiles[step] = context(step)
+                grouped[step] = pick(step)
+            tt = step - 1
+            if 0 <= tt < TILES:
+                accs[tt] = multiply(tt, grouped[tt])
+            tt = step - 2
+            if 0 <= tt < TILES:
+                rounded[tt] = combine(tt, accs[tt], b_tiles[tt], 2 if tt == TILES - 1 else 1)
+            tt = step - 3
+            if 0 <= tt < TILES:
+                hand_on(tt, rounded[tt], 2 if tt == TILES - 1 else 1)
 
         for q in range(4):
             queue = nc.sync if q % 2 == 0 else nc.scalar

@@ -30,24 +30,32 @@ def tile_list_features_by_list_pl_kernel(tc, xt, w_words, w_scales, cx_words, cx
         ps_x = ctx.enter_context(tc.psum_pool(name="ps_x", bufs=1))
         ps_a = ctx.enter_context(tc.psum_pool(name="ps_a", bufs=2))
 
-        def load_words(name, words):
-            tile = keep.tile([P, words.shape[1] // 4], I32, name=name, align_bytes=64)
+        def load_words(name, words, tag):
+            tile = keep.tile([P, words.shape[1] // 4], I32, name=name, tag=tag, align_bytes=64)
             nc.sync.dma_start(tile[:], words.bitcast(I32))
             return tile
 
-        wc_raw = load_words("wc_raw", wc_words[0].rearrange("p n r -> p (n r)"))
-        cx_w = load_words("cx_w", cx_words[0])
-        w_raw = load_words("w_raw", w_words[0].rearrange("p n r -> p (n r)"))
-        offsets = keep.tile([P, I // 16], U16, name="offsets")
-        nc.sync.dma_start(offsets[:], offs)
-        staged = keep.tile([P, 3, 4, P], I32, name="staged")
-        for k, scales in enumerate((wc_scales, w_scales, cx_scales)):
-            nc.sync.dma_start(staged[0:P:32, k, :, :], scales[0].bitcast(I32).rearrange("(q r) c -> q r c", r=4))
-        x_tiles = []
-        for tt in range(TILES):
+        def load_tokens(tt):
             x_tile = keep.tile([P, C], F32, name=f"x{tt}", tag=f"x{tt}", align_bytes=64)
             nc.sync.dma_start(x_tile[:], xt[tt * P:(tt + 1) * P, :])
-            x_tiles.append(x_tile)
+            return x_tile
+
+        def deal(name, raw, dtype, run):
+            dealt = keep.tile([P, N], dtype, name=name, align_bytes=64)
+            nc.vector.tensor_copy(
+                out=dealt[:].rearrange("p (j a b) -> p a j b", j=PACK, b=run),
+                in_=raw.rearrange("p (a b j) -> p a j b", j=PACK, b=run))
+            return dealt
+
+        offsets = keep.tile([P, I // 16], U16, name="offsets")
+        nc.sync.dma_start(offsets[:], offs)
+        staged = keep.tile([P, 3, 4, P], I32, name="staged", tag="x3", align_bytes=64)
+        for k, scales in enumerate((wc_scales, w_scales, cx_scales)):
+            nc.sync.dma_start(staged[0:P:32, k, :, :], scales[0].bitcast(I32).rearrange("(q r) c -> q r c", r=4))
+        wc_raw = load_words("wc_raw", wc_words[0].rearrange("p n r -> p (n r)"), "x1")
+        w_raw = load_words("w_raw", w_words[0].rearrange("p n r -> p (n r)"), "x2")
+        cx_w = load_words("cx_w", cx_words[0], "cx_w")
+        x_tiles = [load_tokens(0)]
 
         planes = keep.tile([P, 3, N], U8, name="planes", align_bytes=64)
         nc.vector.memset(planes[:].bitcast(I32), 0)
@@ -58,16 +66,10 @@ def tile_list_features_by_list_pl_kernel(tc, xt, w_words, w_scales, cx_words, cx
         ident = keep.tile([P, P], F32, name="ident")
         make_identity(nc, ident[:])
 
-        def deal(name, raw, dtype, run):
-            dealt = keep.tile([P, N], dtype, name=name, align_bytes=64)
-            nc.vector.tensor_copy(
-                out=dealt[:].rearrange("p (j a b) -> p a j b", j=PACK, b=run),
-                in_=raw.rearrange("p (a b j) -> p a j b", j=PACK, b=run))
-            return dealt
-
         wc_d = deal("wc_d", wc_raw[:], I32, 4)
-        wc_s = deal("wc_s", planes[:, 0, :], U8, 16)
         w_d = deal("w_d", w_raw[:], I32, 4)
+        x_tiles.extend(load_tokens(tt) for tt in range(1, TILES))
+        wc_s = deal("wc_s", planes[:, 0, :], U8, 16)
         w_s = deal("w_s", planes[:, 1, :], U8, 16)
 
         cx_bytes = cx_w[:].bitcast(U8)
@@ -75,8 +77,8 @@ def tile_list_features_by_list_pl_kernel(tc, xt, w_words, w_scales, cx_words, cx
         out_rows = out_0.rearrange("(p j) t -> p j t", j=PACK)
         out_words = out_1[0].rearrange("p t r -> p (t r)").bitcast(I32)
 
-        def pick(tt):
-            picked = keep.tile([P, I], BF16, name="picked", tag=f"picked{tt}", align_bytes=64)
+        def pick(tt, tag):
+            picked = keep.tile([P, I], BF16, name="picked", tag=tag, align_bytes=64)
             nc.vector.tensor_copy(picked[:], x_tiles[tt][:].indirect(offsets[:]))
             pairs = picked[:].bitcast(F32)
             turned = ps_x.tile([P, 2, P], F32, name="turned", tag=f"bank{tt + 1}")
@@ -99,8 +101,8 @@ def tile_list_features_by_list_pl_kernel(tc, xt, w_words, w_scales, cx_words, cx
             nc.scalar.copy(out=b_tile[:], in_=acc[:])
             return b_tile
 
-        def multiply(tt, grouped):
-            x_codes = keep.tile([P, P], I32, name="x_codes", tag=f"x{tt + 1}", align_bytes=64)
+        def multiply(grouped, tag):
+            x_codes = keep.tile([P, P], I32, name="x_codes", tag=tag, align_bytes=64)
             x_scales = ring.tile([P, P], U8, name="x_scales", align_bytes=64)
             nc.vector.quantize_mx(out=x_codes[:].bitcast(E4M3), scales=x_scales[:], in_=grouped[:])
             acc = ps_a.tile([P, PACK, P], F32, name="acc_a")
@@ -112,9 +114,8 @@ def tile_list_features_by_list_pl_kernel(tc, xt, w_words, w_scales, cx_words, cx
                     start=True, stop=True)
             return acc
 
-        def combine(tt, acc, b_tile, pieces):
-            y = keep.tile([P, PACK, P], F32, name="y", tag=f"grouped{tt + 1}", align_bytes=64)
-            y_grouped = keep.tile([P, P * PACK], BF16, name="y_grouped", tag=f"picked{tt + 2}", align_bytes=64)
+        def combine(tt, acc, b_tile, y_grouped, pieces, tag):
+            y = keep.tile([P, PACK, P], F32, name="y", tag=tag, align_bytes=64)
             width = P // pieces
             for h in range(pieces):
                 part = slice(h * width, (h + 1) * width)
@@ -124,31 +125,41 @@ def tile_list_features_by_list_pl_kernel(tc, xt, w_words, w_scales, cx_words, cx
                 nc.scalar.copy(out=y_grouped[:, PACK * first:PACK * (first + width)].rearrange("p (t j) -> p t j", j=PACK),
                                in_=y[:, :, part].rearrange("p j t -> p t j"))
             nc.sync.dma_start(out_rows[:, :, tt * P:(tt + 1) * P], y[:])
-            return y_grouped
 
-        def hand_on(tt, y_grouped, pieces):
-            y_codes = keep.tile([P, P], I32, name="y_codes", tag=f"b{tt + 1}", align_bytes=64)
-            width = P // pieces
-            for first in range(0, P, width):
-                nc.vector.quantize_mx(out=y_codes[:, first:first + width].bitcast(E4M3),
-                                      scales=y_scales[:, tt * P + first:tt * P + first + width],
-                                      in_=y_grouped[:, PACK * first:PACK * (first + width)])
-            nc.sync.dma_start(out_words[:, tt * P:(tt + 1) * P], y_codes[:])
+        def rounded_tile(tokens, tag):
+            return keep.tile([P, tokens * PACK], BF16, name="y_grouped", tag=tag, align_bytes=64)
 
-        grouped, b_tiles, accs, rounded = {}, {}, {}, {}
-        for step in range(TILES + 3):
-            if step < TILES:
-                b_tiles[step] = context(step)
-                grouped[step] = pick(step)
-            tt = step - 1
-            if 0 <= tt < TILES:
-                accs[tt] = multiply(tt, grouped[tt])
-            tt = step - 2
-            if 0 <= tt < TILES:
-                rounded[tt] = combine(tt, accs[tt], b_tiles[tt], 2 if tt == TILES - 1 else 1)
-            tt = step - 3
-            if 0 <= tt < TILES:
-                hand_on(tt, rounded[tt], 2 if tt == TILES - 1 else 1)
+        def hand_on(first, tokens, y_grouped, pieces, tag):
+            y_codes = keep.tile([P, tokens], I32, name="y_codes", tag=tag, align_bytes=64)
+            width = tokens // pieces
+            for at in range(0, tokens, width):
+                nc.vector.quantize_mx(out=y_codes[:, at:at + width].bitcast(E4M3),
+                                      scales=y_scales[:, first + at:first + at + width],
+                                      in_=y_grouped[:, PACK * at:PACK * (at + width)])
+            nc.sync.dma_start(out_words[:, first:first + tokens], y_codes[:])
+
+        b0 = context(0)
+        grouped0 = pick(0, "picked0")
+        b1 = context(1)
+        grouped1 = pick(1, "picked1")
+        acc0 = multiply(grouped0, "x1")
+        b2 = context(2)
+        grouped2 = pick(2, "picked2")
+        acc1 = multiply(grouped1, "x2")
+        rounded0 = rounded_tile(P, "picked2")
+        combine(0, acc0, b0, rounded0[:], 1, "grouped1")
+        b3 = context(3)
+        grouped3 = pick(3, "picked3")
+        acc2 = multiply(grouped2, "x3")
+        rounded12 = rounded_tile(2 * P, "picked3")
+        combine(1, acc1, b1, rounded12[:, :P * PACK], 1, "grouped2")
+        hand_on(0, P, rounded0, 1, "b1")
+        acc3 = multiply(grouped3, "x_codes3")
+        combine(2, acc2, b2, rounded12[:, P * PACK:], 1, "grouped3")
+        rounded3 = rounded_tile(P, "rounded3")
+        combine(3, acc3, b3, rounded3[:], 2, "y3")
+        hand_on(P, 2 * P, rounded12, 1, "b3")
+        hand_on(3 * P, P, rounded3, 2, "y_codes3")
 
         for q in range(4):
             queue = nc.sync if q % 2 == 0 else nc.scalar

@@ -18,7 +18,16 @@ MULT = mybir.AluOpType.mult
 
 P = 128
 PACK = 4
+QUADRANTS = 4
+SCALE_ROWS = 4
 TILES = T // P
+ROW_WORDS = 512 // 4
+W_PLANE = 8
+LINE = 16
+ALIGN = 64
+
+AREA = 4 * C
+X_CODES_AT, Y_AT, Y_CODES_AT = 1024, 2048, 4096
 
 
 def tile_list_features_by_list_pl_kernel(tc, xt, w_words, w_scales, cx_words, cx_scales, wc_words, wc_scales, offs,
@@ -26,22 +35,24 @@ def tile_list_features_by_list_pl_kernel(tc, xt, w_words, w_scales, cx_words, cx
     nc = tc.nc
     with ExitStack() as ctx:
         keep = ctx.enter_context(tc.tile_pool(name="keep", bufs=1))
+        shared = ctx.enter_context(tc.tile_pool(name="shared", bufs=1))
         ring = ctx.enter_context(tc.tile_pool(name="ring", bufs=2))
-        ps_x = ctx.enter_context(tc.psum_pool(name="ps_x", bufs=1))
+        ps_b = ctx.enter_context(tc.psum_pool(name="ps_b", bufs=PACK))
+        ps_x = ctx.enter_context(tc.psum_pool(name="ps_x", bufs=2))
         ps_a = ctx.enter_context(tc.psum_pool(name="ps_a", bufs=2))
 
-        def load_words(name, words, tag):
-            tile = keep.tile([P, words.shape[1] // 4], I32, name=name, tag=tag, align_bytes=64)
-            nc.sync.dma_start(tile[:], words.bitcast(I32))
+        def load_words(name, packed_bytes, area):
+            tile = shared.tile([P, packed_bytes.shape[1] // 4], I32, name=name, offset=area * AREA, align_bytes=ALIGN)
+            nc.sync.dma_start(tile[:], packed_bytes.bitcast(I32))
             return tile
 
         def load_tokens(tt):
-            x_tile = keep.tile([P, C], F32, name=f"x{tt}", tag=f"x{tt}", align_bytes=64)
+            x_tile = shared.tile([P, C], F32, name=f"x{tt}", offset=tt * AREA, align_bytes=ALIGN)
             nc.sync.dma_start(x_tile[:], xt[tt * P:(tt + 1) * P, :])
             return x_tile
 
         def deal(name, raw, dtype, run):
-            dealt = keep.tile([P, N], dtype, name=name, align_bytes=64)
+            dealt = keep.tile([P, N], dtype, name=name, align_bytes=ALIGN)
             nc.vector.tensor_copy(
                 out=dealt[:].rearrange("p (j a b) -> p a j b", j=PACK, b=run),
                 in_=raw.rearrange("p (a b j) -> p a j b", j=PACK, b=run))
@@ -49,118 +60,126 @@ def tile_list_features_by_list_pl_kernel(tc, xt, w_words, w_scales, cx_words, cx
 
         offsets = keep.tile([P, I // 16], U16, name="offsets")
         nc.sync.dma_start(offsets[:], offs)
-        staged = keep.tile([P, 3, 4, P], I32, name="staged", tag="x3", align_bytes=64)
-        for k, scales in enumerate((wc_scales, w_scales, cx_scales)):
-            nc.sync.dma_start(staged[0:P:32, k, :, :], scales[0].bitcast(I32).rearrange("(q r) c -> q r c", r=4))
-        wc_raw = load_words("wc_raw", wc_words[0].rearrange("p n r -> p (n r)"), "x1")
-        w_raw = load_words("w_raw", w_words[0].rearrange("p n r -> p (n r)"), "x2")
-        cx_w = load_words("cx_w", cx_words[0], "cx_w")
+
+        staged = shared.tile([P, 2, SCALE_ROWS * ROW_WORDS], I32, name="staged", offset=3 * AREA, align_bytes=ALIGN)
+        for scales, place in ((wc_scales, staged[0:P:2 * W_PLANE, 0, :]), (w_scales, staged[W_PLANE:P:2 * W_PLANE, 0, :]),
+                              (cx_scales, staged[0:P:W_PLANE, 1, :])):
+            rows = scales[0].bitcast(I32).rearrange("(q r) c -> q (r c)", r=SCALE_ROWS)
+            copies = place.shape[0] // QUADRANTS
+            nc.sync.dma_start(place, rows.unsqueeze(1).to_broadcast([QUADRANTS, copies, SCALE_ROWS * ROW_WORDS]))
+        wc_raw = load_words("wc_raw", wc_words[0].rearrange("p n r -> p (n r)"), 1)
+        w_raw = load_words("w_raw", w_words[0].rearrange("p n r -> p (n r)"), 2)
+        cx_w = load_words("cx_w", cx_words[0], TILES)
         x_tiles = [load_tokens(0)]
 
-        planes = keep.tile([P, 3, N], U8, name="planes", align_bytes=64)
+        planes = keep.tile([P, 2, N], U8, name="planes", align_bytes=ALIGN)
         nc.vector.memset(planes[:].bitcast(I32), 0)
-        for r in range(4):
-            nc.scalar.dma_start(planes[:].bitcast(I32)[r:P:32, :, :], staged[0:P:32, :, r, :])
-        cx_s = planes[:, 2, :]
+        for r in range(SCALE_ROWS):
+            nc.scalar.dma_start(planes[:].bitcast(I32)[r:P:W_PLANE, :, :],
+                                staged[0:P:W_PLANE, :, r * ROW_WORDS:(r + 1) * ROW_WORDS])
+        cx_plane = planes[:, 1, :]
 
         ident = keep.tile([P, P], F32, name="ident")
         make_identity(nc, ident[:])
 
-        wc_d = deal("wc_d", wc_raw[:], I32, 4)
-        w_d = deal("w_d", w_raw[:], I32, 4)
+        wc_dealt = deal("wc_dealt", wc_raw[:], I32, LINE // 4)
+        w_dealt = deal("w_dealt", w_raw[:], I32, LINE // 4)
         x_tiles.extend(load_tokens(tt) for tt in range(1, TILES))
-        wc_s = deal("wc_s", planes[:, 0, :], U8, 16)
-        w_s = deal("w_s", planes[:, 1, :], U8, 16)
+        weight_planes = deal("weight_planes", planes[:, 0, :], U8, LINE)
 
-        cx_bytes = cx_w[:].bitcast(U8)
-        y_scales = keep.tile([P, T], U8, name="y_scales", align_bytes=64)
+        y_scales = keep.tile([P, T], U8, name="y_scales", align_bytes=ALIGN)
         out_rows = out_0.rearrange("(p j) t -> p j t", j=PACK)
         out_words = out_1[0].rearrange("p t r -> p (t r)").bitcast(I32)
 
-        def pick(tt, tag):
-            picked = keep.tile([P, I], BF16, name="picked", tag=tag, align_bytes=64)
+        def pick(tt):
+            picked = keep.tile([P, I], BF16, name="picked", tag=f"picked{tt}", align_bytes=ALIGN)
             nc.vector.tensor_copy(picked[:], x_tiles[tt][:].indirect(offsets[:]))
             pairs = picked[:].bitcast(F32)
-            turned = ps_x.tile([P, 2, P], F32, name="turned", tag=f"bank{tt + 1}")
+            turned = ps_x.tile([P, 2, P], F32, name="turned")
             for u in range(2):
                 nc.tensor.transpose(turned[:, u, :], pairs[:, u::2], ident[:])
-            grouped = keep.tile([P, P * PACK], BF16, name="grouped", tag=f"grouped{tt}", align_bytes=64)
+            grouped = keep.tile([P, P * PACK], BF16, name="grouped", tag=f"grouped{tt}", align_bytes=ALIGN)
             nc.scalar.copy(out=grouped[:].bitcast(F32).rearrange("p (t u) -> p t u", u=2),
                            in_=turned[:].rearrange("p u t -> p t u"))
             return grouped
 
-        def context(tt):
-            acc = ps_x.tile([P, PACK, P], F32, name="acc_b", tag=f"bank{tt}")
+        def context():
+            b_all = keep.tile([P, PACK, T], F32, name="b_all", tag="b_all", align_bytes=ALIGN)
             for j in range(PACK):
+                acc_b = ps_b.tile([P, T], F32, name="acc_b")
                 nc.tensor.matmul_mx(
-                    out=acc[:, j, :],
-                    lhsT=wc_d[:, j * P:(j + 1) * P].bitcast(E4M3), lhsT_scale=wc_s[:, j * P:(j + 1) * P],
-                    rhs=cx_bytes[:, 2 * tt * P:2 * (tt + 1) * P].bitcast(E2M1), rhs_scale=cx_s[:, tt * P:(tt + 1) * P],
+                    out=acc_b[:],
+                    lhsT=wc_dealt[:, j * P:(j + 1) * P].bitcast(E4M3), lhsT_scale=weight_planes[:, j * P:(j + 1) * P],
+                    rhs=cx_w[:].bitcast(U8).bitcast(E2M1), rhs_scale=cx_plane,
                     start=True, stop=True)
-            b_tile = keep.tile([P, PACK, P], F32, name=f"b{tt}", tag=f"b{tt}", align_bytes=64)
-            nc.scalar.copy(out=b_tile[:], in_=acc[:])
-            return b_tile
+                nc.scalar.copy(out=b_all[:, j, :], in_=acc_b[:])
+            return b_all
 
-        def multiply(grouped, tag):
-            x_codes = keep.tile([P, P], I32, name="x_codes", tag=tag, align_bytes=64)
-            x_scales = ring.tile([P, P], U8, name="x_scales", align_bytes=64)
+        def multiply(tt, grouped):
+            x_codes = shared.tile([P, P], I32, name=f"x_codes{tt}", offset=(tt + 1) * AREA + X_CODES_AT, align_bytes=ALIGN)
+            x_scales = ring.tile([P, P], U8, name="x_scales", align_bytes=ALIGN)
             nc.vector.quantize_mx(out=x_codes[:].bitcast(E4M3), scales=x_scales[:], in_=grouped[:])
-            acc = ps_a.tile([P, PACK, P], F32, name="acc_a")
+            acc_a = ps_a.tile([P, PACK, P], F32, name="acc_a")
             for j in range(PACK):
                 nc.tensor.matmul_mx(
-                    out=acc[:, j, :],
-                    lhsT=w_d[:, j * P:(j + 1) * P].bitcast(E4M3), lhsT_scale=w_s[:, j * P:(j + 1) * P],
+                    out=acc_a[:, j, :],
+                    lhsT=w_dealt[:, j * P:(j + 1) * P].bitcast(E4M3),
+                    lhsT_scale=weight_planes[W_PLANE:P, j * P:(j + 1) * P],
                     rhs=x_codes[:].bitcast(E4M3), rhs_scale=x_scales[:],
                     start=True, stop=True)
-            return acc
+            return acc_a
 
-        def combine(tt, acc, b_tile, y_grouped, pieces, tag):
-            y = keep.tile([P, PACK, P], F32, name="y", tag=tag, align_bytes=64)
+        def combine(tt, acc_a, y, rounded, pieces):
             width = P // pieces
-            for h in range(pieces):
-                part = slice(h * width, (h + 1) * width)
-                nc.vector.scalar_tensor_tensor(out=y[:, :, part], in0=acc[:, :, part], scalar=0.0, in1=b_tile[:, :, part],
-                                               op0=MAX, op1=MULT)
-                first = h * width
-                nc.scalar.copy(out=y_grouped[:, PACK * first:PACK * (first + width)].rearrange("p (t j) -> p t j", j=PACK),
+            for first in range(0, P, width):
+                part = slice(first, first + width)
+                nc.vector.scalar_tensor_tensor(out=y[:, :, part], in0=acc_a[:, :, part], scalar=0.0,
+                                               in1=b_all[:, :, tt * P + first:tt * P + first + width], op0=MAX, op1=MULT)
+                nc.scalar.copy(out=rounded[:, PACK * first:PACK * (first + width)].rearrange("p (t j) -> p t j", j=PACK),
                                in_=y[:, :, part].rearrange("p j t -> p t j"))
             nc.sync.dma_start(out_rows[:, :, tt * P:(tt + 1) * P], y[:])
 
-        def rounded_tile(tokens, tag):
-            return keep.tile([P, tokens * PACK], BF16, name="y_grouped", tag=tag, align_bytes=64)
-
-        def hand_on(first, tokens, y_grouped, pieces, tag):
-            y_codes = keep.tile([P, tokens], I32, name="y_codes", tag=tag, align_bytes=64)
+        def hand_on(first_token, rounded, y_codes, pieces):
+            tokens = y_codes.shape[1]
             width = tokens // pieces
-            for at in range(0, tokens, width):
-                nc.vector.quantize_mx(out=y_codes[:, at:at + width].bitcast(E4M3),
-                                      scales=y_scales[:, first + at:first + at + width],
-                                      in_=y_grouped[:, PACK * at:PACK * (at + width)])
-            nc.sync.dma_start(out_words[:, first:first + tokens], y_codes[:])
+            for first in range(0, tokens, width):
+                nc.vector.quantize_mx(out=y_codes[:, first:first + width].bitcast(E4M3),
+                                      scales=y_scales[:, first_token + first:first_token + first + width],
+                                      in_=rounded[:, PACK * first:PACK * (first + width)])
+            nc.sync.dma_start(out_words[:, first_token:first_token + tokens], y_codes[:])
 
-        b0 = context(0)
-        grouped0 = pick(0, "picked0")
-        b1 = context(1)
-        grouped1 = pick(1, "picked1")
-        acc0 = multiply(grouped0, "x1")
-        b2 = context(2)
-        grouped2 = pick(2, "picked2")
-        acc1 = multiply(grouped1, "x2")
-        rounded0 = rounded_tile(P, "picked2")
-        combine(0, acc0, b0, rounded0[:], 1, "grouped1")
-        b3 = context(3)
-        grouped3 = pick(3, "picked3")
-        acc2 = multiply(grouped2, "x3")
-        rounded12 = rounded_tile(2 * P, "picked3")
-        combine(1, acc1, b1, rounded12[:, :P * PACK], 1, "grouped2")
-        hand_on(0, P, rounded0, 1, "b1")
-        acc3 = multiply(grouped3, "x_codes3")
-        combine(2, acc2, b2, rounded12[:, P * PACK:], 1, "grouped3")
-        rounded3 = rounded_tile(P, "rounded3")
-        combine(3, acc3, b3, rounded3[:], 2, "y3")
-        hand_on(P, 2 * P, rounded12, 1, "b3")
-        hand_on(3 * P, P, rounded3, 2, "y_codes3")
+        grouped0 = pick(0)
+        b_all = context()
+        grouped1 = pick(1)
+        acc0 = multiply(0, grouped0)
 
-        for q in range(4):
+        grouped2 = pick(2)
+        acc1 = multiply(1, grouped1)
+        y0 = shared.tile([P, PACK, P], F32, name="y0", offset=2 * AREA + Y_AT, align_bytes=ALIGN)
+        rounded0 = keep.tile([P, P * PACK], BF16, name="rounded0", tag="picked2", align_bytes=ALIGN)
+        combine(0, acc0, y0, rounded0[:], pieces=1)
+
+        grouped3 = pick(3)
+        acc2 = multiply(2, grouped2)
+        y1 = shared.tile([P, PACK, P], F32, name="y1", offset=3 * AREA + Y_AT, align_bytes=ALIGN)
+        rounded12 = keep.tile([P, 2 * P * PACK], BF16, name="rounded12", tag="picked3", align_bytes=ALIGN)
+        combine(1, acc1, y1, rounded12[:, :P * PACK], pieces=1)
+        y_codes0 = shared.tile([P, P], I32, name="y_codes0", offset=3 * AREA + Y_CODES_AT, align_bytes=ALIGN)
+        hand_on(0, rounded0, y_codes0, pieces=1)
+
+        acc3 = multiply(3, grouped3)
+        y2 = keep.tile([P, PACK, P], F32, name="y2", tag="grouped3", align_bytes=ALIGN)
+        combine(2, acc2, y2, rounded12[:, P * PACK:], pieces=1)
+
+        rounded3 = keep.tile([P, P * PACK], BF16, name="rounded3", align_bytes=ALIGN)
+        y3 = keep.tile([P, PACK, P], F32, name="y3")
+        combine(3, acc3, y3, rounded3[:], pieces=2)
+        y_codes12 = keep.tile([P, 2 * P], I32, name="y_codes12", tag="b_all", align_bytes=ALIGN)
+        hand_on(P, rounded12, y_codes12, pieces=1)
+        y_codes3 = keep.tile([P, P], I32, name="y_codes3", align_bytes=ALIGN)
+        hand_on(3 * P, rounded3, y_codes3, pieces=2)
+
+        for q in range(QUADRANTS):
             queue = nc.sync if q % 2 == 0 else nc.scalar
-            queue.dma_start(out_2[0, 4 * q:4 * q + 4, :].bitcast(I32), y_scales[32 * q:32 * q + 4, :].bitcast(I32))
+            queue.dma_start(out_2[0, SCALE_ROWS * q:SCALE_ROWS * (q + 1), :].bitcast(I32),
+                            y_scales[32 * q:32 * q + SCALE_ROWS, :].bitcast(I32))

from contextlib import ExitStack

import concourse.mybir as mybir
from concourse.masks import make_identity

C, I, T, L, N = 2048, 512, 512, 512, 512
FLOPS = 2 * N * T * (I + L)

F32 = mybir.dt.float32
BF16 = mybir.dt.bfloat16
I32 = mybir.dt.int32
U16 = mybir.dt.uint16
U8 = mybir.dt.uint8
E4M3 = mybir.dt.float8_e4m3fn_x4
E2M1 = mybir.dt.float4_e2m1fn_x4
MAX = mybir.AluOpType.max
MULT = mybir.AluOpType.mult

P = 128
PACK = 4
QUADRANTS = 4
SCALE_ROWS = 4
TILES = T // P
ROW_WORDS = 512 // 4
W_PLANE = 8
LINE = 16
ALIGN = 64

AREA = 4 * C
X_CODES_AT, Y_AT, Y_CODES_AT = 1024, 2048, 4096


def tile_list_features_by_list_pl_kernel(tc, xt, w_words, w_scales, cx_words, cx_scales, wc_words, wc_scales, offs,
                                            out_0, out_1, out_2):
    nc = tc.nc
    with ExitStack() as ctx:
        keep = ctx.enter_context(tc.tile_pool(name="keep", bufs=1))
        shared = ctx.enter_context(tc.tile_pool(name="shared", bufs=1))
        ring = ctx.enter_context(tc.tile_pool(name="ring", bufs=2))
        ps_b = ctx.enter_context(tc.psum_pool(name="ps_b", bufs=PACK))
        ps_x = ctx.enter_context(tc.psum_pool(name="ps_x", bufs=2))
        ps_a = ctx.enter_context(tc.psum_pool(name="ps_a", bufs=2))

        def load_words(name, packed_bytes, area):
            tile = shared.tile([P, packed_bytes.shape[1] // 4], I32, name=name, offset=area * AREA, align_bytes=ALIGN)
            nc.sync.dma_start(tile[:], packed_bytes.bitcast(I32))
            return tile

        def load_tokens(tt):
            x_tile = shared.tile([P, C], F32, name=f"x{tt}", offset=tt * AREA, align_bytes=ALIGN)
            nc.sync.dma_start(x_tile[:], xt[tt * P:(tt + 1) * P, :])
            return x_tile

        def deal(name, raw, dtype, run):
            dealt = keep.tile([P, N], dtype, name=name, align_bytes=ALIGN)
            nc.vector.tensor_copy(
                out=dealt[:].rearrange("p (j a b) -> p a j b", j=PACK, b=run),
                in_=raw.rearrange("p (a b j) -> p a j b", j=PACK, b=run))
            return dealt

        offsets = keep.tile([P, I // 16], U16, name="offsets")
        nc.sync.dma_start(offsets[:], offs)

        staged = shared.tile([P, 2, SCALE_ROWS * ROW_WORDS], I32, name="staged", offset=3 * AREA, align_bytes=ALIGN)
        for scales, place in ((wc_scales, staged[0:P:2 * W_PLANE, 0, :]), (w_scales, staged[W_PLANE:P:2 * W_PLANE, 0, :]),
                              (cx_scales, staged[0:P:W_PLANE, 1, :])):
            rows = scales[0].bitcast(I32).rearrange("(q r) c -> q (r c)", r=SCALE_ROWS)
            copies = place.shape[0] // QUADRANTS
            nc.sync.dma_start(place, rows.unsqueeze(1).to_broadcast([QUADRANTS, copies, SCALE_ROWS * ROW_WORDS]))
        wc_raw = load_words("wc_raw", wc_words[0].rearrange("p n r -> p (n r)"), 1)
        w_raw = load_words("w_raw", w_words[0].rearrange("p n r -> p (n r)"), 2)
        cx_w = load_words("cx_w", cx_words[0], TILES)
        x_tiles = [load_tokens(0)]

        planes = keep.tile([P, 2, N], U8, name="planes", align_bytes=ALIGN)
        nc.vector.memset(planes[:].bitcast(I32), 0)
        for r in range(SCALE_ROWS):
            nc.scalar.dma_start(planes[:].bitcast(I32)[r:P:W_PLANE, :, :],
                                staged[0:P:W_PLANE, :, r * ROW_WORDS:(r + 1) * ROW_WORDS])
        cx_plane = planes[:, 1, :]

        ident = keep.tile([P, P], F32, name="ident")
        make_identity(nc, ident[:])

        wc_dealt = deal("wc_dealt", wc_raw[:], I32, LINE // 4)
        w_dealt = deal("w_dealt", w_raw[:], I32, LINE // 4)
        x_tiles.extend(load_tokens(tt) for tt in range(1, TILES))
        weight_planes = deal("weight_planes", planes[:, 0, :], U8, LINE)

        y_scales = keep.tile([P, T], U8, name="y_scales", align_bytes=ALIGN)
        out_rows = out_0.rearrange("(p j) t -> p j t", j=PACK)
        out_words = out_1[0].rearrange("p t r -> p (t r)").bitcast(I32)

        def pick(tt):
            picked = keep.tile([P, I], BF16, name="picked", tag=f"picked{tt}", align_bytes=ALIGN)
            nc.vector.tensor_copy(picked[:], x_tiles[tt][:].indirect(offsets[:]))
            pairs = picked[:].bitcast(F32)
            turned = ps_x.tile([P, 2, P], F32, name="turned")
            for u in range(2):
                nc.tensor.transpose(turned[:, u, :], pairs[:, u::2], ident[:])
            grouped = keep.tile([P, P * PACK], BF16, name="grouped", tag=f"grouped{tt}", align_bytes=ALIGN)
            nc.scalar.copy(out=grouped[:].bitcast(F32).rearrange("p (t u) -> p t u", u=2),
                           in_=turned[:].rearrange("p u t -> p t u"))
            return grouped

        def context():
            b_all = keep.tile([P, PACK, T], F32, name="b_all", tag="b_all", align_bytes=ALIGN)
            for j in range(PACK):
                acc_b = ps_b.tile([P, T], F32, name="acc_b")
                nc.tensor.matmul_mx(
                    out=acc_b[:],
                    lhsT=wc_dealt[:, j * P:(j + 1) * P].bitcast(E4M3), lhsT_scale=weight_planes[:, j * P:(j + 1) * P],
                    rhs=cx_w[:].bitcast(U8).bitcast(E2M1), rhs_scale=cx_plane,
                    start=True, stop=True)
                nc.scalar.copy(out=b_all[:, j, :], in_=acc_b[:])
            return b_all

        def multiply(tt, grouped):
            x_codes = shared.tile([P, P], I32, name=f"x_codes{tt}", offset=(tt + 1) * AREA + X_CODES_AT, align_bytes=ALIGN)
            x_scales = ring.tile([P, P], U8, name="x_scales", align_bytes=ALIGN)
            nc.vector.quantize_mx(out=x_codes[:].bitcast(E4M3), scales=x_scales[:], in_=grouped[:])
            acc_a = ps_a.tile([P, PACK, P], F32, name="acc_a")
            for j in range(PACK):
                nc.tensor.matmul_mx(
                    out=acc_a[:, j, :],
                    lhsT=w_dealt[:, j * P:(j + 1) * P].bitcast(E4M3),
                    lhsT_scale=weight_planes[W_PLANE:P, j * P:(j + 1) * P],
                    rhs=x_codes[:].bitcast(E4M3), rhs_scale=x_scales[:],
                    start=True, stop=True)
            return acc_a

        def combine(tt, acc_a, y, rounded, pieces):
            width = P // pieces
            for first in range(0, P, width):
                part = slice(first, first + width)
                nc.vector.scalar_tensor_tensor(out=y[:, :, part], in0=acc_a[:, :, part], scalar=0.0,
                                               in1=b_all[:, :, tt * P + first:tt * P + first + width], op0=MAX, op1=MULT)
                nc.scalar.copy(out=rounded[:, PACK * first:PACK * (first + width)].rearrange("p (t j) -> p t j", j=PACK),
                               in_=y[:, :, part].rearrange("p j t -> p t j"))
            nc.sync.dma_start(out_rows[:, :, tt * P:(tt + 1) * P], y[:])

        def hand_on(first_token, rounded, y_codes, pieces):
            tokens = y_codes.shape[1]
            width = tokens // pieces
            for first in range(0, tokens, width):
                nc.vector.quantize_mx(out=y_codes[:, first:first + width].bitcast(E4M3),
                                      scales=y_scales[:, first_token + first:first_token + first + width],
                                      in_=rounded[:, PACK * first:PACK * (first + width)])
            nc.sync.dma_start(out_words[:, first_token:first_token + tokens], y_codes[:])

        grouped0 = pick(0)
        b_all = context()
        grouped1 = pick(1)
        acc0 = multiply(0, grouped0)

        grouped2 = pick(2)
        acc1 = multiply(1, grouped1)
        y0 = shared.tile([P, PACK, P], F32, name="y0", offset=2 * AREA + Y_AT, align_bytes=ALIGN)
        rounded0 = keep.tile([P, P * PACK], BF16, name="rounded0", tag="picked2", align_bytes=ALIGN)
        combine(0, acc0, y0, rounded0[:], pieces=1)

        grouped3 = pick(3)
        acc2 = multiply(2, grouped2)
        y1 = shared.tile([P, PACK, P], F32, name="y1", offset=3 * AREA + Y_AT, align_bytes=ALIGN)
        rounded12 = keep.tile([P, 2 * P * PACK], BF16, name="rounded12", tag="picked3", align_bytes=ALIGN)
        combine(1, acc1, y1, rounded12[:, :P * PACK], pieces=1)
        y_codes0 = shared.tile([P, P], I32, name="y_codes0", offset=3 * AREA + Y_CODES_AT, align_bytes=ALIGN)
        hand_on(0, rounded0, y_codes0, pieces=1)

        acc3 = multiply(3, grouped3)
        y2 = keep.tile([P, PACK, P], F32, name="y2", tag="grouped3", align_bytes=ALIGN)
        combine(2, acc2, y2, rounded12[:, P * PACK:], pieces=1)

        rounded3 = keep.tile([P, P * PACK], BF16, name="rounded3", align_bytes=ALIGN)
        y3 = keep.tile([P, PACK, P], F32, name="y3")
        combine(3, acc3, y3, rounded3[:], pieces=2)
        y_codes12 = keep.tile([P, 2 * P], I32, name="y_codes12", tag="b_all", align_bytes=ALIGN)
        hand_on(P, rounded12, y_codes12, pieces=1)
        y_codes3 = keep.tile([P, P], I32, name="y_codes3", align_bytes=ALIGN)
        hand_on(3 * P, rounded3, y_codes3, pieces=2)

        for q in range(QUADRANTS):
            queue = nc.sync if q % 2 == 0 else nc.scalar
            queue.dma_start(out_2[0, SCALE_ROWS * q:SCALE_ROWS * (q + 1), :].bitcast(I32),
                            y_scales[32 * q:32 * q + SCALE_ROWS, :].bitcast(I32))
